import numpy as np, ml_dtypes
CORES = [10,34,74,98]
N = 4
import mx_ref
BF = ml_dtypes.bfloat16
def entries(a):
    return np.ascontiguousarray(a.T).reshape(-1)
def table(e):
    return np.ascontiguousarray(np.reshape(e, (-1, 16)).T).astype(np.int32)
def cols(t, e):
    v = np.concatenate([t.reshape(128, -1, 4), np.zeros((128, 1, 4), BF)], axis=1)
    return np.ascontiguousarray(v[:, e]).reshape(128, -1)
def f(rng, *shape):
    return mx_ref.flush((rng.standard_normal(shape, dtype=np.float32) * np.exp2(rng.integers(-2, 3, shape[:-1] + (1,)))).astype(BF))
def wide(rng, *shape, cols=0):
    v = rng.standard_normal(shape, dtype=np.float32) * np.exp2(rng.integers(-12, 13, shape)).astype(np.float32)
    if cols: v *= np.repeat(np.exp2(rng.integers(-cols, cols + 1, shape[:-2] + (1, shape[-1] // 4))) * (rng.random(shape[:-2] + (1, shape[-1] // 4)) > 0.0625), 4, axis=-1).astype(np.float32)
    return mx_ref.flush(v.astype(BF))
T, CAPP = 512, 192
def lists(rng, full=False, skew=False, single=False, back=False):
    if full:
        v = rng.permutation(([CAPP] * (T // CAPP) + [T % CAPP] + [0] * N)[:N])
        n = v[(np.arange(N)[None, :] - np.arange(N)[:, None]) % N][rng.permutation(N)][:, rng.permutation(N)]
    else:
        n = np.full((N, N), T // N)
        for _ in range(20 * N):
            (s, t), (d, e) = rng.permutation(N)[:2], rng.permutation(N)[:2]
            k = rng.integers(0, min(n[s, d], n[t, e], CAPP - n[s, e], CAPP - n[t, d]) + 1)
            n[s, d] -= k; n[t, e] -= k; n[s, e] += k; n[t, d] += k
    a = np.full((N, N * CAPP), -1)
    for s in range(N):
        parts = np.split(rng.permutation(T), np.cumsum(n[s])[:-1])
        for d in range(N): a[s, d * CAPP + rng.permutation(CAPP)[:n[s, d]]] = parts[d]
    p, u, o = [], [], []
    for r in range(N):
        used = np.flatnonzero(a[:, r * CAPP:(r + 1) * CAPP].reshape(-1) >= 0)
        p.append(table(used[::-1] if back else rng.permutation(used)))
        h = rng.integers(0, N)
        c = rng.integers(0, 2, N) if full else (np.full(N, -1) if rng.random() < 0.5 else rng.integers(0, 2, N)) if single else rng.integers(-1, 2, N)
        if c[h] < 0: c[h] = rng.integers(0, 2)
        named = np.flatnonzero(c >= 0)
        if single: named = np.array([h])
        if skew:
            m = rng.integers(T // 2 + 1, T + 1)
            e = np.sort(np.concatenate([np.full(m, h), rng.choice(named, T - m)]))
        elif full: e = np.sort(np.concatenate([named, rng.choice(named, T - N)]))
        else: e = np.repeat(named, np.diff(np.concatenate([[0], np.sort(rng.integers(0, T + 1, len(named) - 1)), [T]])))
        u.append(table(np.concatenate([c, np.full(16 - N, -1)]))); o.append(table(e))
    return {"send": np.stack([table(k) for k in a]), "place": np.stack(p), "sel": np.stack(u), "of": np.stack(o)}
def setup_inputs(rng):
    return {"x": f(rng, N, 128, 4 * T), "w": f(rng, N, 256, 512), **lists(rng)}
def setup_inputs_full(rng):
    return {**setup_inputs(rng), **lists(rng, full=True)}
def setup_inputs_reversed(rng):
    return {**setup_inputs(rng), **lists(rng, back=True)}
def setup_inputs_single(rng):
    return {**setup_inputs(rng), **lists(rng, single=True)}
def setup_inputs_skew(rng):
    return {**setup_inputs(rng), **lists(rng, skew=True)}
def setup_inputs_spread(rng):
    d = setup_inputs(rng); d["x"] = wide(rng, N, 128, 4 * T, cols=8); return d
def check_inputs(d):
    b = []
    for k in ("x", "w"):
        a = np.abs(d[k].astype(np.float32))
        if not ((a == 0) | ((a >= 2.0 ** -30) & (a <= 2.0 ** 30))).all(): b.append(k)
    sends = np.stack([entries(d["send"][r]) for r in range(N)])
    for r in range(N):
        c, p, u, e = sends[r], entries(d["place"][r]), entries(d["sel"][r]), entries(d["of"][r])
        if c.min() < -1 or not np.array_equal(np.sort(c[c >= 0]), np.arange(T)): b.append("send")
        if not np.array_equal(np.sort(p), np.flatnonzero(sends[:, r * CAPP:(r + 1) * CAPP].reshape(-1) >= 0)): b.append("place")
        if u.min() < -1 or u.max() > 1 or (u[N:] != -1).any(): b.append("sel")
        if e.min() < 0 or e.max() >= N or (np.diff(e) < 0).any() or (u[e] < 0).any(): b.append("of")
    return b
def reference(x, w, send, place, sel, of):
    W = [[mx_ref.quantize(w[h][128 * m:128 * m + 128]) for m in range(2)] for h in range(N)]
    y = np.zeros((N, 128, T), np.float32)
    for r in range(N):
        slots = np.concatenate([cols(x[s], entries(send[s])[r * CAPP:(r + 1) * CAPP]) for s in range(N)], axis=1)
        X = mx_ref.quantize(cols(slots, entries(place[r])))
        u, e = entries(sel[r]), entries(of[r])
        for h in range(N):
            i = e == h
            if i.any(): y[r][:, i] = mx_ref.matmul(W[h][u[h]], X)[:, i]
    return {"y": y}

from concourse.bass import DstId, RemoteDMATransfer
from concourse.mybir import dt, AluOpType, ActivationFunctionType

N, COLS, CAP, F = 4, 512, 192, 128
PAIR = 2 * CAP
ALL = N * CAP
EXPERTS = 6
CODES = "float8_e4m3fn_x4"

SCRATCH = {
    "xs": ("sbuf", [128, 4 * COLS], "bfloat16"),
    "ws": ("sbuf", [128, 8 * F], "bfloat16"),
    "slist": ("sbuf", [128, N * CAP // 16], "int32"),
    "seli": ("sbuf", [128, 16], "int32"),
    "po": ("sbuf", [16, 64], "int32"),
    "ip": ("sbuf", [128, 32], "int32"),
    "ia": ("sbuf", [128, 32], "int32"),
    "ic": ("sbuf", [128, 32], "int32"),
    "jj": ("sbuf", [128, 32], "float32"),
    "self_": ("sbuf", [128, 16], "float32"),
    "selb": ("sbuf", [128, 4], "float32"),
    "selin": ("sbuf", [128, 4], "float32"),
    "ox": ("sbuf", [128, N * CAP // 16], "uint16"),
    "oe": ("sbuf", [128, 64], "uint16"),
    "base": ("sbuf", [16, 2], "float32"),
    "oa": ("sbuf", [16, 128], "float32"),
    "ob": ("sbuf", [16, 128], "float32"),
    "off1": ("sbuf", [16, 32], "uint16"),
    "off": ("sbuf", [128, 32], "uint16"),
    "xtq": ("sbuf", [128, 4 * PAIR], "bfloat16"),
    "xtp": ("sbuf", [128, 4 * CAP], "bfloat16"),
    "xto": ("sbuf", [128, 4 * CAP], "bfloat16"),
    "et": ("sbuf", [128, 8 * F], "bfloat16"),
    "eco": ("sbuf", [128, 2 * F], CODES),
    "xcp": ("sbuf", [128, CAP], CODES),
    "spp": ("sbuf", [128, CAP + 2 * F], "uint8"),
    "xcq": ("sbuf", [128, PAIR], CODES),
    "ecq": ("sbuf", [128, 2 * F], CODES),
    "sql": ("sbuf", [128, CAP + F], "uint8"),
    "sqh": ("sbuf", [128, CAP + F], "uint8"),
    "xc1": ("sbuf", [128, PAIR], CODES),
    "epc": ("sbuf", [128, 2 * F], CODES),
    "sc1": ("sbuf", [128, PAIR + 2 * F], "uint8"),
    "xc2": ("sbuf", [128, PAIR], CODES),
    "eqc": ("sbuf", [128, 2 * F], CODES),
    "sc2": ("sbuf", [128, PAIR + 2 * F], "uint8"),
    "hx": ("sbuf", [128, CAP], CODES),
    "ps": ("psum", [128, 4096], "float32"),
    "res": ("sbuf", [128, EXPERTS * ALL], "float32"),
    "yb": ("sbuf", [128, COLS], "float32"),
}
SEMAPHORES = ["l_sel", "l_list", "l_w", "l_x", "l_po", "l_off",
              "e_i1", "e_i2", "e_ia", "e_j", "e_self", "e_selb", "e_ox", "e_E",
              "e_gq", "e_xq", "e_gp", "e_xp", "e_oe", "e_ge", "e_e", "e_go", "e_xo",
              "e_base", "e_m", "e_s1", "e_s2", "e_s3", "e_off",
              "selarr", "parr", "eql", "eqh", "xq", "hin", "sent",
              "e_yv", "e_ys", "st"] + ["mm%d" % k for k in range(12)] + ["cp%d" % k for k in range(12)]


def u8(view):
    return view.bitcast(dt.uint8)


def bits(engines):
    return sum(1 << e for e in engines)


def helpers(r, T, topo):
    c = T.cores[r]
    l = 2 * (1 - r // 2)
    other = [k for k in topo.cores_of(c) if topo.die(k) != topo.die(c)]
    out = {}
    for d in sorted((l, l + 1), key=lambda d: sum(topo.may_write(k, T.cores[d]) for k in other)):
        k = [k for k in other if topo.may_write(k, T.cores[d]) and k not in out.values()][0]
        out[d] = k
    return out


def hand_on(g, core, T, topo, s, d):
    dst = T.cores[d]
    rid, pid, _ = topo.addr(dst)
    n = len(topo.engines(core, dst))
    a = (s % 2) * CAP
    g.wait_ge(T.sem.hin, 8)
    g.remote_dma(u8(T.xc2[:, a:a + CAP]), u8(T.hx[:]), T.sem.xq, T.sem.sent, pid, rid, topo.mask(core, dst))
    g.wait_ge(T.sem.sent, n)


def rank_program(g, core, T, topo):
    r = T.rank_of(core)
    if r is None:
        for s in range(N):
            for d, k in helpers(s, T, topo).items():
                if k == core:
                    hand_on(g, core, T, topo, s, d)
        return
    S, v, sc, te, sy = T.sem, g.vector, g.scalar, g.tensor, g.sync
    A, COPY = AluOpType, ActivationFunctionType.Copy
    p, l = r ^ 1, 2 * (1 - r // 2)
    h = l + 1
    odd = r % 2
    dst = {d: T.cores[d] for d in (p, l, h)}
    help_ = helpers(r, T, topo)
    sent = [0]

    def one(out, in_, sem, d, mask, n):
        rid, pid, _ = topo.addr(d)
        g.remote_dma(out, in_, sem, S.sent, pid, rid, mask)
        sent[0] += n

    def two(items):
        tr = []
        for i, (out, in_, sem, d) in enumerate(items):
            en = topo.engines(core, d)
            half = en[:len(en) // 2] if i == 0 else en[len(en) // 2:]
            rid, pid, _ = topo.addr(d)
            tr.append(RemoteDMATransfer(dst_ids=[DstId(rid=rid, pnc=pid)], dma_engine_mask=bits(half), remote_sem=sem, src=in_, dst=out))
            sent[0] += len(half)
        g.remote_dma_fused(tr, local_sem=S.sent)

    spp_e, spp_x = (CAP, 0) if odd else (0, 2 * F)
    sq_e, sq_x = (CAP, 0) if odd else (0, F)
    if odd:
        sc1_e, sc1_x, own = 0, 2 * F, CAP
    else:
        sc1_e, sc1_x, own = PAIR, 0, 0
    land_p = CAP if odd else 0
    land_sp = CAP if odd else 0
    land_sq = (CAP + F) if odd else 0
    land_e = F if odd else 0

    sc.dma_start(T.seli[0:1, 0:16], T.sel[:]).then_inc(S.l_sel, 16)
    for k in range(4):
        sc.dma_start(T.slist[16 * k:16 * k + 16, :], T.send[:]).then_inc(S.l_list, 16)
    sc.dma_start(T.xs[:], T.x[:]).then_inc(S.l_x, 16)
    sy.dma_start(T.ws[:, 0:512], T.w[0:128, :]).then_inc(S.l_w, 16)
    sy.dma_start(T.ws[:, 512:1024], T.w[128:256, :]).then_inc(S.l_w, 16)
    for k in range(4, 8):
        sy.dma_start(T.slist[16 * k:16 * k + 16, :], T.send[:]).then_inc(S.l_list, 16)
    sy.dma_start(T.po[:, 0:32], T.place[:]).then_inc(S.l_po, 16)
    sy.dma_start(T.po[:, 32:64], T.of[:]).then_inc(S.l_po, 16)

    g.iota(T.ip[:], [[0, 32]], 0, 1).then_inc(S.e_i1, 1)
    g.iota(T.ic[:], [[16, 32]], 0, 0).then_inc(S.e_i2, 1)
    g.wait_ge(S.e_self, 1)
    g.partition_broadcast(T.selb[:, 0:4], T.self_[0:1, 0:4], 128).then_inc(S.e_selb, 1)
    g.wait_ge(S.e_selb, 1)
    two([(T.selin[:, odd:odd + 1], T.selb[:, d:d + 1], S.selarr, dst[d]) for d in (l, h)])
    m = topo.mask(core, dst[p])
    n = len(topo.engines(core, dst[p]))
    g.wait_ge(S.e_E, 1)
    one(u8(T.epc[:]), u8(T.eco[:]), S.parr, dst[p], m, n)
    g.wait_ge(S.e_xq, 2)
    two([(u8(T.hx[:]), u8(T.xcq[:, i * CAP:(i + 1) * CAP]), S.hin, help_[d]) for i, d in enumerate((l, h))])
    g.wait_ge(S.e_xp, 1)
    one(u8(T.xc1[:, land_p:land_p + CAP]), u8(T.xcp[:]), S.parr, dst[p], m, n)
    one(T.sc1[:, land_sp:land_sp + CAP + 2 * F], T.spp[:], S.parr, dst[p], m, n)
    g.wait_ge(S.e_e, 2)
    esem = S.eqh if odd else S.eql
    two([(u8(T.eqc[:, land_e:land_e + F]), u8(T.ecq[:, i * F:(i + 1) * F]), esem, dst[d]) for i, d in enumerate((l, h))])
    two([(T.sc2[:, land_sq:land_sq + CAP + F], q[:], esem, dst[d]) for q, d in ((T.sql, l), (T.sqh, h))])
    g.wait_ge(S.sent, sent[0])

    v.wait_ge(S.e_i1, 1)
    v.tensor_scalar(T.ia[:], T.ip[:], 15, None, A.bitwise_and).then_inc(S.e_ia, 1)
    v.wait_ge(S.e_i2, 1)
    v.wait_ge(S.e_ia, 1)
    v.tensor_tensor(T.jj[:], T.ia[:], T.ic[:], A.add).then_inc(S.e_j, 1)
    v.wait_ge(S.l_sel, 16)
    v.tensor_scalar(T.self_[0:1, :], T.seli[0:1, :], 512.0, 0.0, A.mult, A.max).then_inc(S.e_self, 1)
    v.wait_ge(S.l_list, 128)
    v.tensor_scalar(T.ox[:], T.slist[:], 4.0, 0.0, A.mult, A.max).then_inc(S.e_ox, 1)
    v.wait_ge(S.l_w, 32)
    v.quantize_mx(T.eco[:], T.spp[:, spp_e:spp_e + 2 * F], T.ws[:]).then_inc(S.e_E, 1)

    def gather(tile, n, first, sem):
        o = T.ox[:, first // 16:(first + n) // 16]
        for t in range(2):
            v.tensor_copy(tile[:, t:4 * n:4], T.xs[:, t:4 * COLS].indirect(o)).then_inc(sem, 1)
        for t in range(2, 4):
            sc.activation(tile[:, t:4 * n:4], T.xs[:, t:4 * COLS].indirect(o), COPY).then_inc(sem, 1)
        v.wait_ge(sem, 4)

    for q in (v, sc):
        q.wait_ge(S.l_x, 16)
        q.wait_ge(S.e_ox, 1)
    gather(T.xtq, PAIR, l * CAP, S.e_gq)
    for i, q in enumerate((T.sql, T.sqh)):
        v.quantize_mx(T.xcq[:, i * CAP:(i + 1) * CAP], q[:, sq_x:sq_x + CAP], T.xtq[:, 4 * i * CAP:4 * (i + 1) * CAP]).then_inc(S.e_xq, 1)
    gather(T.xtp, CAP, p * CAP, S.e_gp)
    v.quantize_mx(T.xcp[:], T.spp[:, spp_x:spp_x + CAP], T.xtp[:]).then_inc(S.e_xp, 1)
    v.wait_ge(S.selarr, 8)
    v.wait_ge(S.e_j, 1)
    for i in range(2):
        v.tensor_scalar(T.oe[:, 32 * i:32 * i + 32], T.jj[:], T.selin[:, i:i + 1], None, A.add).then_inc(S.e_oe, 1)
    for q in (v, sc):
        q.wait_ge(S.e_oe, 2)
    sc.wait_ge(S.l_w, 32)
    v.tensor_copy(T.et[:, 0:512], T.ws[:, 0:1024].indirect(T.oe[:, 0:32])).then_inc(S.e_ge, 1)
    sc.activation(T.et[:, 512:1024], T.ws[:, 0:1024].indirect(T.oe[:, 32:64]), COPY).then_inc(S.e_ge, 1)
    v.wait_ge(S.e_ge, 2)
    for i, q in enumerate((T.sql, T.sqh)):
        v.quantize_mx(T.ecq[:, i * F:(i + 1) * F], q[:, sq_e:sq_e + F], T.et[:, 512 * i:512 * (i + 1)]).then_inc(S.e_e, 1)
    gather(T.xto, CAP, r * CAP, S.e_go)
    so = sc1_x + own
    v.quantize_mx(T.xc1[:, own:own + CAP], T.sc1[:, so:so + CAP], T.xto[:]).then_inc(S.e_xo, 1)
    v.wait_ge(S.l_po, 32)
    v.wait_ge(S.e_selb, 1)
    v.tensor_scalar(T.base[:, 0:1], T.selb[0:16, r:r + 1], ALL / 512.0, None, A.mult).then_inc(S.e_base, 1)
    v.tensor_scalar(T.base[:, 1:2], T.selb[0:16, p:p + 1], ALL / 512.0, 2.0 * ALL, A.mult, A.add).then_inc(S.e_base, 1)
    v.wait_ge(S.e_base, 2)
    of, place = T.po[:, 32:64], T.po[:, 0:32]
    for i, (who, b) in enumerate(((r, T.base[:, 0:1]), (p, T.base[:, 1:2]), (l, 4.0 * ALL), (h, 5.0 * ALL))):
        v.tensor_scalar(T.oa[:, 32 * i:32 * i + 32], of, float(who), b, A.is_equal, A.mult).then_inc(S.e_m, 1)
    v.wait_ge(S.e_m, 4)
    v.tensor_tensor(T.ob[:, 0:64], T.oa[:, 0:64], T.oa[:, 64:128], A.add).then_inc(S.e_s1, 1)
    v.wait_ge(S.e_s1, 1)
    v.tensor_tensor(T.ob[:, 64:96], T.ob[:, 0:32], T.ob[:, 32:64], A.add).then_inc(S.e_s2, 1)
    v.wait_ge(S.e_s2, 1)
    v.tensor_tensor(T.ob[:, 96:128], T.ob[:, 64:96], place, A.add).then_inc(S.e_s3, 1)
    v.wait_ge(S.e_s3, 1)
    v.tensor_copy(T.off1[:], T.ob[:, 96:128]).then_inc(S.e_off, 1)
    sy.wait_ge(S.e_off, 1)
    for k in range(8):
        sy.dma_start(T.off[16 * k:16 * k + 16, :], T.off1[:]).then_inc(S.l_off, 16)

    def expert(e):
        a = (e % 2) * F
        if e < 2:
            return T.eco[:, a:a + F], T.spp[:, spp_e + a:spp_e + a + F]
        if e < 4:
            return T.epc[:, a:a + F], T.sc1[:, sc1_e + a:sc1_e + a + F]
        b = 0 if e == 4 else F + PAIR
        return T.eqc[:, a:a + F], T.sc2[:, b:b + F]
    group = {0: (T.xc1[:], T.sc1[:, sc1_x:sc1_x + PAIR], r // 2), 1: (T.xc2[:], T.sc2[:, F:F + PAIR], 1 - r // 2)}
    own_w, p_w, l_w, h_w, x_w = (S.e_E, 1), (S.parr, 3 * n), (S.eql, 8), (S.eqh, 8), (S.xq, 16)
    order = [(0, 0, [own_w, p_w, (S.e_xo, 1)]), (1, 0, []), (2, 0, []), (3, 0, []),
             (4, 0, [l_w]), (5, 0, [h_w]), (4, 1, [x_w]), (5, 1, []), (0, 1, []), (1, 1, []), (2, 1, []), (3, 1, [])]
    for k, (e, gr, waits) in enumerate(order):
        for sem, val in waits:
            te.wait_ge(sem, val)
        if k >= 8:
            te.wait_ge(S["cp%d" % (k - 8)], 1)
        bank = 512 * (k % 8)
        W, Ws = expert(e)
        X, Xs, pos = group[gr]
        te.matmul_mx(T.ps[:, bank:bank + PAIR], W, Ws, X, Xs, True, True).then_inc(S["mm%d" % k], 1)
        q = sc if k % 2 else v
        q.wait_ge(S["mm%d" % k], 1)
        o = T.res[:, e * ALL + pos * PAIR:e * ALL + (pos + 1) * PAIR]
        if k % 2:
            sc.activation(o, T.ps[:, bank:bank + PAIR], COPY).then_inc(S["cp%d" % k], 1)
        else:
            v.tensor_copy(o, T.ps[:, bank:bank + PAIR]).then_inc(S["cp%d" % k], 1)

    for q in (v, sc):
        q.wait_ge(S.l_off, 128)
        for k in range(12):
            q.wait_ge(S["cp%d" % k], 1)
    v.tensor_copy(T.yb[:, 0:256], T.res[:].indirect(T.off[:, 0:16])).then_inc(S.e_yv, 1)
    sc.activation(T.yb[:, 256:512], T.res[:].indirect(T.off[:, 16:32]), COPY).then_inc(S.e_ys, 1)
    sy.wait_ge(S.e_yv, 1)
    sy.dma_start(T.y[:, 0:256], T.yb[:, 0:256]).then_inc(S.st, 16)
    sc.wait_ge(S.e_ys, 1)
    sc.dma_start(T.y[:, 256:512], T.yb[:, 256:512]).then_inc(S.st, 16)
    sy.wait_ge(S.st, 32)
